import numpy as np, ml_dtypes
CORES = [6,15,38,47]
N = 4
BF = ml_dtypes.bfloat16
def gentries(a):
    return np.ascontiguousarray(a.reshape(8, 16, -1).transpose(0, 2, 1)).reshape(8, -1)
def gtable(e):
    e = np.asarray(e); return np.ascontiguousarray(e.reshape(8, -1, 16).transpose(0, 2, 1)).reshape(128, -1).astype(np.int32)
LV, M, V, Q = 2, 4, 7, 1
C, S, T, U = 2048, 4096, 1024, 640
def glists(e):
    return np.stack([gtable(e[r]) for r in range(N)])
def slots(rng):
    return np.argsort(rng.random((N, 8, N, C)), axis=-1)[..., :U]
def setup_inputs(rng):
    x = (0.125 + 0.875 * rng.random((N, 128, M * C), dtype=np.float32)).astype(BF)
    tr = (0.5 * rng.random((N, 128, 16 * (V + 1)), dtype=np.float32) ** 3).astype(BF)
    mp = rng.integers(0, C, (N, 8, (V - 1) * S)).astype(np.int32)
    rep = glists(rng.integers(0, S, (N, 8, (M - 1) * C)))
    uc = glists(slots(rng).reshape(N, 8, N * U))
    ps = glists(rng.integers(0, U, (N, 8, S)))
    return {"x": x, "tr": tr, "mp": mp, "rep": rep, "uc": uc, "ps": ps}
def setup_inputs_ends(rng):
    d = setup_inputs(rng)
    e = rng.integers(0, S, (N, 8, (M - 1) * C)); e = np.where(rng.random(e.shape) < 0.4, rng.choice(np.array([0, 1, S - 2, S - 1]), e.shape), e); e[:, :, 0] = S - 1; e[:, :, -1] = 0
    m = rng.integers(0, C, (N, 8, V - 1, S)); m = np.where(rng.random(m.shape) < 0.3, rng.choice(np.array([0, 1, C - 2, C - 1]), m.shape), m); m[..., 0] = C - 1; m[..., -1] = 0
    u = slots(rng); u[..., 0] = C - 1; u[..., -1] = 0
    p = rng.integers(0, U, (N, 8, N, T)); p = np.where(rng.random(p.shape) < 0.3, rng.choice(np.array([0, U - 1]), p.shape), p); p[..., 0] = U - 1; p[..., -1] = 0
    d["rep"] = glists(e); d["mp"] = m.reshape(N, 8, (V - 1) * S).astype(np.int32); d["uc"] = glists(u.reshape(N, 8, N * U)); d["ps"] = glists(p.reshape(N, 8, S)); return d
def setup_inputs_full(rng):
    d = setup_inputs(rng); p = np.concatenate([np.broadcast_to(np.arange(U), (N, 8, N, U)), rng.integers(0, U, (N, 8, N, T - U))], axis=-1)
    p = np.take_along_axis(p, np.argsort(rng.random(p.shape), axis=-1), -1)
    d["ps"] = glists(p.reshape(N, 8, S)); return d
def setup_inputs_alike(rng):
    d = setup_inputs(rng); a = int(rng.integers(0, N)); b = (a + 1) % N; c = (a + 2) % N
    e = gentries(d["rep"][a]); e[rng.integers(0, 8)] = rng.integers(0, S); d["rep"][a] = gtable(e)
    d["uc"][b] = gtable(np.repeat(rng.integers(0, C, (8, N)), U, axis=1))
    d["ps"][c] = gtable(np.repeat(rng.integers(0, U, (8, N)), T, axis=1)); return d
def setup_inputs_spread(rng):
    d = setup_inputs(rng); k = np.exp2(rng.integers(-2, 3, (N, 8, 1, C))) * (rng.random((N, 8, 1, C)) > 0.0625)
    x = d["x"].astype(np.float32).reshape(N, 8, 16, M * C); x[..., :C] *= k.astype(np.float32)
    d["x"] = x.reshape(N, 128, M * C).astype(BF); return d
def largest(x, t):
    P = t.astype(np.float64).reshape(N, 8, 16, V + 1, 16).transpose(0, 1, 3, 4, 2); top = x.reshape(N, 8, 16, M, C).max(axis=-1).astype(np.float64)
    X = [top[..., v] for v in range(M)]; seen = list(X)
    def times(p, v):
        return np.matmul(p, v[..., None])[..., 0]
    for k in range(M - 1):
        a, b = times(P[:, :, 2 * k], X[2 * k]), times(P[:, :, 2 * k + 1], X[2 * k + 1])
        X.append(a * b); seen += [a, b, a * b]
    Z = times(P[:, :, V - 1], X[V - 1]); seen.append(Z)
    for q in range(N):
        for k in range(Q):
            for a, b, c, e in ((0, 1, 2, 3), (0, 2, 1, 3), (0, 3, 1, 2)):
                h = Z[4 * k + a] * Z[4 * k + b]; l = Z[4 * k + c] * Z[4 * k + e]; w = times(P[q, :, V], l)
                seen += [h, l, w, np.sum(h * w, axis=-1)]
    return np.max(np.array([np.max(v) for v in seen]))
def check_inputs(d):
    bad = []
    try:
        x, t = np.asarray(d["x"]).astype(np.float32), np.asarray(d["tr"]).astype(np.float32)
        if not (np.isfinite(x).all() and (x >= 0).all() and (x <= 64).all()): bad.append("x")
        if not ((t >= 0) & (t <= 1)).all(): bad.append("tr")
        if not bad and not largest(x, t) < 2.0 ** 120: bad.append("size")
        for name, top in (("mp", C), ("rep", S), ("uc", C), ("ps", U)):
            a = np.asarray(d[name])
            if not ((a >= 0) & (a < top)).all(): bad.append(name)
    except Exception:
        bad.append("form")
    return bad
def reference(x, tr, mp, rep, uc, ps):
    z = np.zeros((N, 8, 16, C), np.float64); y = np.zeros((N, 8, Q, 3, T), np.float64)
    P = np.ascontiguousarray(tr.astype(np.float64).reshape(N, 8, 16, V + 1, 16).transpose(0, 1, 3, 4, 2))
    for r in range(N):
        leaf = x[r].astype(np.float64).reshape(8, 16, M, C); m = mp[r].reshape(8, V - 1, S); e = gentries(rep[r]).reshape(8, M - 1, C)
        for g in range(8):
            X = [leaf[g, :, v] for v in range(M)]
            for k in range(M - 1):
                a, b = 2 * k, 2 * k + 1; s = e[g, k]
                X.append((P[r, g, a] @ X[a])[:, m[g, a][s]] * (P[r, g, b] @ X[b])[:, m[g, b][s]])
            z[r, g] = P[r, g, V - 1] @ X[V - 1]
    u = [gentries(uc[r]).reshape(8, N, U) for r in range(N)]; p = [gentries(ps[r]).reshape(8, N, T) for r in range(N)]
    for q in range(N):
        w = P[q, :, V]; Z = []
        for r in range(N):
            c = np.take_along_axis(u[r][:, q], p[r][:, q], 1)
            Z.append(np.stack([z[r, g][:, c[g]] for g in range(8)]))
        for k in range(Q):
            for t, (a, b, c, d) in enumerate(((0, 1, 2, 3), (0, 2, 1, 3), (0, 3, 1, 2))):
                h = Z[4 * k + a] * Z[4 * k + b]; l = Z[4 * k + c] * Z[4 * k + d]
                y[q, :, k, t] = np.sum(h * np.matmul(w, l), axis=1)
    return {"y": y.reshape(N, 8, Q * 3 * T).astype(np.float32)}

from concourse.bass import DstId, RemoteDMATransfer
from concourse.mybir import AluOpType, ActivationFunctionType

N, C, S, TS, U = 4, 2048, 4096, 1024, 640
F32, BF16, I32, U16 = "float32", "bfloat16", "int32", "uint16"

SCRATCH = {
    "trs": ("sbuf", [128, 8, 16], BF16),
    "xs": ("sbuf", [128, 4 * C], BF16),
    "win": ("sbuf", [128, S], I32),
    "reps": ("sbuf", [128, 24, 16], I32),
    "repu": ("sbuf", [128, 384], U16),
    "ucs": ("sbuf", [128, 10, 16], I32),
    "ucf": ("sbuf", [128, 10, 16], F32),
    "ucu": ("sbuf", [128, 160], U16),
    "ex": ("sbuf", [128, 26, 128], F32),
    "pss": ("sbuf", [128, 256], I32),
    "psu": ("sbuf", [128, 256], U16),
    "pso": ("sbuf", [128, 256], U16),
    "mask": ("sbuf", [128, 8], F32),
    "ee": ("sbuf", [128, 72], F32),
    "si": ("sbuf", [128, 160], I32),
    "sj": ("sbuf", [128, 160], I32),
    "sl": ("sbuf", [128, 160], F32),
    "ident": ("sbuf", [128, 128], F32),
    "lb": ("sbuf", [128, 4, 128], BF16),
    "lf": ("sbuf", [128, 4, 128], F32),
    "wt": ("sbuf", [128, 128], F32),
    "gi": ("sbuf", [128, 2 * C], U16),
    "offs": ("sbuf", [128, 512], U16),
    "g2": ("sbuf", [128, C], F32),
    "hf": ("sbuf", [128, N * U], F32),
    "hc": ("sbuf", [128, 320], F32),
    "o6": ("sbuf", [128, 320], U16),
    "aa": ("sbuf", [128, 6 * C], F32),
    "tmp": ("sbuf", [128, 2 * C], F32),
    "xj": ("sbuf", [128, 2 * C], F32),
    "tmp6": ("sbuf", [128, N * U], F32),
    "x6": ("sbuf", [128, N * U], F32),
    "zout": ("sbuf", [128, 3 * U], F32),
    "zin": ("sbuf", [128, N * U], F32),
    "mz": ("sbuf", [128, 3 * TS], F32),
    "fin": ("sbuf", [128, 3 * TS], F32),
    "red": ("sbuf", [128, 192], F32),
    "outs": ("sbuf", [128, 384], F32),
}
for _b in range(8):
    SCRATCH["pm%d" % _b] = ("psum", [128, 512], F32)

SEMAPHORES = ["cv", "cs", "cp", "cg", "d_tr", "d_x0", "d_x1", "d_x2", "d_x3", "d_x4", "d_rep", "d_rep2", "d_map",
              "d_uc", "d_ps", "r0", "r1", "r2", "r3", "h0", "h1", "d_y", "a_ps", "a0", "a1", "a2", "sent"]

JOINS = ((0, 1, 2, 3), (0, 2, 1, 3), (0, 3, 1, 2))
ROW = (0, 4, 8, 12, 1, 9)
PW = 320
NP = U // PW
FILL = 2784

ORDER = {
    "v": "fillv ex1 ex2 ex5 s1 ex7 s2 ex4 ex6 ex0 ex3 uf ux4 ux3 xc0 ux5 i0 xc1 i1 i2 rep2 ucc i3 psc j2 t0 t1 lc14"
         " t2 lc12 t3 g6 t5 t6 g7 t4 t7 c2 ho0 c4 c7 ho1 t6_0_0 t6_0_1 t6_3_1 g6_1_1 t6_1_0 t6_1_1 t6_3_0 g6_2_0 wt"
         " t6_2_0 t6_2_1 m0_1 cz_2_1 p0_0 p0_1 p2_0 p1_1 p2_1 p1_0"
         " l0_0 l0_1 f0_0 l1_0 f0_1 f1_0 l1_1 l2_0 f1_1 f2_0 l2_1 f2_1 f2_2",
    "s": "ld_tr m1 ld_x0 m0 m2 lb4 lb3 lb1 lb6 lb5 lb7 lb2 lb0 lf0 lf6 lf4 lf5 lf2 lf1 lf3 lf7 lc0 lc1"
         " ux1 ux6 ux7 ux0 ux2 lc2 lc3 lc4 lc5 lc6 lc7 lc8 lc10 g0 g1 lc11 g2 lc9 g3 lc15 g5 lc13 g4 h0 h1"
         " c1 c0 c5 c3 c6 g6_0_0 g6_0_1 g6_3_1 g6_1_0 cz_0_0 cz_0_1 g6_3_0 cz_3_1 g6_2_1 cz_1_0 cz_1_1 cz_3_0"
         " m0_0 cz_2_0 m1_1 m1_0 m2_1 m2_0 rc0 oc0 rc1 rc2 oc1 oc2",
    "p": "lm0 lm1 xm0 xm1 lm3 lm2 um lm4 lm5 lm7 lm6 lm8 lm10 lm9 lm11 lm14 lm13 lm12 lm15"
         " jm0 jm1 jm2 jm3 jm5 jm6 jm4 jm7 zm_0_0 zm_0_1 zm_3_1 zm_1_0 zm_1_1 zm_3_0 zm_2_0 zm_2_1"
         " w0_0 w0_1 w2_0 w1_1 w2_1 w1_0 rm0_0 rm0_1 rm1_0 tp0 rm1_1 rm2_0 tp1 tp2 dm0 dm1",
    "y": "ld_rep ld_uc ld_map ld_x1 ld_x2 ld_rep2 ld_x3 ld_ps rl0 rl1 ld_x4 rl2 rl3 rh0 rh1 st0 st1 st2",
    "g": "ones fillg s0a s0b id0 e0 id1 e1 e2 sps sz0 sz1 sz2",
}


def seq(fmt, rng):
    return [fmt % i for i in rng]


def orders():
    return {q: ORDER[q].split() for q in ORDER}


def rank_program(g, core, T, topo):
    rank = T.rank_of(core)
    if rank is None:
        return
    cores = list(T.cores)
    me = topo.chip(core)

    def hops(r):
        ch = topo.chip(cores[r])
        return 0 if topo.mates(me, ch) else (1 if topo.same_plane(me, ch) else 2)

    peers = sorted([r for r in range(N) if r != rank], key=hops)
    blocks = peers + [rank]
    halves = [blocks[0] // 2, 1 - blocks[0] // 2]
    Q = {"v": g.vector, "s": g.scalar, "p": g.tensor, "y": g.sync, "g": g}
    CSEM = {"v": "cv", "s": "cs", "p": "cp", "g": "cg"}
    mult = AluOpType.mult
    Act = ActivationFunctionType
    PM = [T["pm%d" % b] for b in range(8)]
    ops = {}

    def comp(name, deps, fn):
        ops[name] = ("c", deps, fn, None)

    def dma(name, deps, pairs, sem):
        ops[name] = ("d", deps, pairs, sem)

    def copy(q, out, in_):
        return q.tensor_copy(out, in_) if q is g.vector else q.activation(out, in_, Act.Copy)

    def masked(q, out, in_, k):
        col = T.mask[:, k:k + 1]
        if q is g.vector:
            return q.tensor_scalar(out, in_, col, None, mult)
        return q.activation(out, in_, Act.Identity, scale=col)

    comp("ones", [], lambda q: q.iota(T.mask[:], [[-32, 8]], -15, 2, allow_small_or_imprecise_dtypes=True))
    comp("m1", ["ones"], lambda q: q.activation(T.mask[:], T.mask[:], Act.Abs))
    comp("m0", ["m1"], lambda q: q.activation(T.mask[:], T.mask[:], Act.Sign, bias=16.0, scale=-1.0))
    comp("m2", ["m0"], lambda q: q.activation(T.mask[:], T.mask[:], Act.Relu))
    comp("fillg", [], lambda q: q.iota(T.win[:, FILL:S], [[0, S - FILL]], 0, 0))
    comp("fillv", [], lambda q: q.memset(T.win[:, 0:FILL], 0))
    comp("e0", [], lambda q: q.iota(T.ee[:], [[0, 72]], 1, 0, allow_small_or_imprecise_dtypes=True))
    comp("e1", ["e0"], lambda q: q.affine_select(T.ee[:], T.ee[:], [[-16, 9], [1000, 8]], AluOpType.is_ge, 0.0, -7000, 1))
    comp("e2", ["e1"], lambda q: q.affine_select(T.ee[:], T.ee[:], [[16, 9], [0, 8]], AluOpType.is_ge, 0.0, 15, -1))
    comp("id0", [], lambda q: q.iota(T.ident[:], [[0, 128]], 1, 0, allow_small_or_imprecise_dtypes=True))
    comp("id1", ["id0"], lambda q: q.affine_select(T.ident[:], T.ident[:], [[-1, 128]], AluOpType.is_equal, 0.0, 0, 1))
    comp("s0a", [], lambda q: q.iota(T.si[:, 0:68], [[-8, 17], [1, 4]], 1024 - 3, 8))
    comp("s0b", [], lambda q: q.iota(T.si[:, 68:153], [[-8, 17], [1, 5]], 1024 - 4, 8))
    comp("s1", ["s0a", "s0b"], lambda q: q.tensor_scalar(T.sj[:, 0:153], T.si[:, 0:153], 127, None, AluOpType.bitwise_and))
    comp("s2", ["s1"], lambda q: q.tensor_scalar(T.sl[:, 0:153], T.sj[:, 0:153], 0.0, None, AluOpType.is_equal))

    dma("ld_tr", [], [(T.trs[:], T.tr[:])], "d_tr")
    dma("ld_x0", [], [(T.xs[:, 0:1024], T.x[:, 0:1024])], "d_x0")
    dma("ld_x1", [], [(T.xs[:, 1024:C], T.x[:, 1024:C])], "d_x1")
    for v in (1, 2, 3):
        dma("ld_x%d" % (v + 1), [], [(T.xs[:, C * v:C * (v + 1)], T.x[:, C * v:C * (v + 1)])], "d_x%d" % (v + 1))
    dma("ld_rep", [], [(T.reps[:, 0:16, :], T.rep[:, 0:256])], "d_rep")
    dma("ld_rep2", [], [(T.reps[:, 16:24, :], T.rep[:, 256:384])], "d_rep2")
    dma("ld_map", ["fillv", "fillg"],
        [(T.win[ROW[0]:128:4, :], T.mp[:, 0:4 * S]), (T.win[ROW[4]:128:8, :], T.mp[:, 4 * S:6 * S])], "d_map")
    dma("ld_uc", [], [(T.ucs[:], T.uc[:])], "d_uc")
    dma("ld_ps", [], [(T.pss[:], T.ps[:])], "d_ps")

    for k in range(8):
        cols = slice(16 * k, 16 * k + 16)
        comp("lb%d" % k, ["ld_tr", "m2"], lambda q, k=k, cols=cols: masked(q, T.lb[:, :, cols], T.trs[:, 0:4, :], k))
        comp("lf%d" % k, ["ld_tr", "m2"], lambda q, k=k, cols=cols: masked(q, T.lf[:, :, cols], T.trs[:, 4:8, :], k))
        comp("ex%d" % k, ["ld_rep", "m2"], lambda q, k=k, cols=cols: masked(q, T.ex[:, 0:16, cols], T.reps[:, 0:16, :], k))
        comp("ux%d" % k, ["uf", "m2"], lambda q, k=k, cols=cols: masked(q, T.ex[:, 16:26, cols], T.ucf[:], k))
    LB, LF, EX, UX = (seq(n + "%d", range(8)) for n in ("lb", "lf", "ex", "ux"))
    comp("wt", LF, lambda q: q.transpose(T.wt[:], T.lf[:, 3, :]))
    comp("uf", ["ld_uc"], lambda q: q.tensor_copy(T.ucf[:], T.ucs[:]))

    reader = {"xm0": "xc0", "xm1": "xc1", "um": "ucc"}
    for i in range(16):
        reader["lm%d" % i] = "lc%d" % i
    for i in range(8):
        reader["jm%d" % i] = "c%d" % i
    for n in range(N):
        for i in range(NP):
            reader["zm_%d_%d" % (n, i)] = "cz_%d_%d" % (n, i)
    turn = [name for name in orders()["p"] if name in reader]
    free = [reader[[name for i, name in enumerate(turn) if i % 8 == b][-1]] for b in range(8)]

    def bank(name):
        i = turn.index(name)
        return PM[i % 8], ([reader[turn[i - 8]]] if i >= 8 else [])

    for i in range(16):
        v = i // 4
        pm, war = bank("lm%d" % i)
        ld = "ld_x%d" % (i // 2 if v == 0 else v + 1)
        comp("lm%d" % i, LB + [ld] + war, lambda q, i=i, v=v, pm=pm: q.matmul(
            pm[:], T.lb[:, v, :], T.xs[:, 512 * i:512 * i + 512], True, True))
        comp("lc%d" % i, ["lm%d" % i], lambda q, i=i, pm=pm: copy(q, T.aa[:, 512 * i:512 * i + 512], pm[:]))

    def node(v):
        return seq("lc%d", range(4 * v, 4 * v + 4)) if v < 4 else seq("c%d", range(4 * (v - 4), 4 * (v - 4) + 4))

    def window(v):
        return T.aa[:, C * v:C * (v + 1)]

    def turn_lists(q, pm, first, chunks, w, at):
        last = None
        for c in range(chunks):
            for b in range(w):
                last = q.matmul(pm[:, 16 * w * c:16 * w * (c + 1)], T.ex[:, first + w * c + b, :],
                                T.sl[:, at + w - 1 - b:at + w - 1 - b + 16 * w], b == 0, b == w - 1)
        return last

    for name, rd, deps, first, chunks, w, at, out in (
            ("xm0", "xc0", EX, 0, 1, 4, 0, T.repu[:, 0:64]), ("xm1", "xc1", EX, 4, 3, 4, 0, T.repu[:, 64:256]),
            ("um", "ucc", UX, 16, 2, 5, 68, T.ucu[:])):
        pm, war = bank(name)
        comp(name, deps + ["s2"] + war, lambda q, pm=pm, first=first, chunks=chunks, w=w, at=at: turn_lists(
            q, pm, first, chunks, w, at))
        comp(rd, [name], lambda q, pm=pm, out=out, n=16 * w * chunks: q.tensor_copy(out, pm[:, 0:n]))
    comp("rep2", ["ld_rep2"], lambda q: q.tensor_copy(T.repu[:, 256:384], T.reps[:, 16:24, :]))
    comp("psc", ["ld_ps"], lambda q: q.tensor_copy(T.psu[:], T.pss[:]))
    for i in range(4):
        k, h = i // 2, i % 2
        comp("i%d" % i, ["ld_map", "xc%d" % min(i, 1)], lambda q, i=i: q.tensor_copy(
            T.gi[:, 1024 * i:1024 * i + 1024], T.win[:, 0:S].indirect(T.repu[:, 64 * i:64 * i + 64])))
        dma("rl%d" % i, ["i%d" % i],
            [(T.offs[:, 128 * v + 64 * h:128 * v + 64 * h + 64], T.gi[ROW[v]:128:16, 1024 * i:1024 * i + 1024])
             for v in (2 * k, 2 * k + 1)], "r%d" % i)
    comp("j2", ["ld_map", "rep2"], lambda q: q.tensor_copy(T.g2[:], T.win[:, 0:S].indirect(T.repu[:, 256:384])))

    for i in range(8):
        k, j = i // 4, i % 4
        rl = "rl%d" % (i // 2)
        oa, ob = 256 * k + 32 * j, 256 * k + 128 + 32 * j
        cols = slice(512 * i, 512 * i + 512)
        comp("g%d" % i, node(2 * k) + [rl], lambda q, k=k, oa=oa, cols=cols: copy(
            q, T.tmp[:, cols], window(2 * k).indirect(T.offs[:, oa:oa + 32])))
        comp("t%d" % i, node(2 * k + 1) + [rl, "g%d" % i], lambda q, k=k, ob=ob, cols=cols: q.tensor_tensor(
            T.xj[:, cols], window(2 * k + 1).indirect(T.offs[:, ob:ob + 32]), T.tmp[:, cols], mult))
        pm, war = bank("jm%d" % i)
        comp("jm%d" % i, LF + ["t%d" % i] + war, lambda q, k=k, pm=pm, cols=cols: q.matmul(
            pm[:], T.lf[:, k, :], T.xj[:, cols], True, True))
        comp("c%d" % i, ["jm%d" % i], lambda q, i=i, pm=pm: copy(
            q, T.aa[:, 4 * C + 512 * i:4 * C + 512 * i + 512], pm[:]))

    for n in range(2):
        h = halves[n]
        comp("h%d" % n, ["j2", "ucc"], lambda q, h=h: copy(
            q, T.hf[:, 2 * U * h:2 * U * (h + 1)], T.g2[:, 0:C].indirect(T.ucu[:, 80 * h:80 * h + 80])))
        dma("rh%d" % n, ["h%d" % n],
            [(T.hc[:, 160 * h + 80 * a:160 * h + 80 * a + 80], T.hf[ROW[4 + a]:128:16, 2 * U * h:2 * U * (h + 1)])
             for a in range(2)], "h%d" % n)
        comp("ho%d" % n, ["rh%d" % n], lambda q, h=h: q.tensor_copy(
            T.o6[:, 160 * h:160 * h + 160], T.hc[:, 160 * h:160 * h + 160]))
    for n in range(N):
        blk = blocks[n]
        ho = "ho%d" % halves.index(blk // 2)
        for i in range(NP):
            tag = "_%d_%d" % (n, i)
            w = PW // 16
            oa = 160 * (blk // 2) + 40 * (blk % 2) + w * i
            cols = slice(U * n + PW * i, U * n + PW * i + PW)
            comp("g6" + tag, node(4) + [ho], lambda q, oa=oa, cols=cols, w=w: copy(
                q, T.tmp6[:, cols], window(4).indirect(T.o6[:, oa:oa + w])))
            comp("t6" + tag, node(5) + [ho, "g6" + tag], lambda q, oa=oa, cols=cols, w=w: q.tensor_tensor(
                T.x6[:, cols], window(5).indirect(T.o6[:, oa + 80:oa + 80 + w]), T.tmp6[:, cols], mult))
            pm, war = bank("zm" + tag)
            comp("zm" + tag, ["t6" + tag] + war, lambda q, pm=pm, cols=cols: q.matmul(
                pm[:, 0:PW], T.lf[:, 2, :], T.x6[:, cols], True, True))
            dst = T.zout[:, cols] if n < 3 else T.zin[:, U * rank + PW * i:U * rank + PW * i + PW]
            comp("cz" + tag, ["zm" + tag], lambda q, pm=pm, dst=dst: copy(q, dst, pm[:, 0:PW]))

    def made(n):
        return ["cz_%d_%d" % (n, i) for i in range(NP)]

    eng = topo.engines(core, cores[peers[0]])
    half, quarter = len(eng) // 2, len(eng) // 4
    parts = [eng[:half], eng[half:half + quarter], eng[half + quarter:]]
    sent = [0]

    def send_ps(q):
        trs = []
        for n in range(3):
            rid, pid, _ = topo.addr(cores[peers[n]])
            trs.append(RemoteDMATransfer(
                dst_ids=[DstId(rid=rid, pnc=pid)], dma_engine_mask=sum(1 << e for e in parts[n]),
                remote_sem=T.sem.a_ps, src=T.psu[:, 64 * peers[n]:64 * peers[n] + 64],
                dst=T.pso[:, 64 * rank:64 * rank + 64]))
        q.remote_dma_fused(trs, local_sem=T.sem.sent)
        sent[0] += len(eng)

    ops["sps"] = ("r", ["psc"], send_ps, None)
    for n in range(3):
        def send_z(q, n=n):
            dst = cores[peers[n]]
            rid, pid, _ = topo.addr(dst)
            q.remote_dma(T.zin[:, U * rank:U * rank + U], T.zout[:, U * n:U * n + U], T.sem["a%d" % n], T.sem.sent,
                         pid, rid, topo.mask(core, dst))
            sent[0] += len(topo.engines(core, dst))
        ops["sz%d" % n] = ("r", made(n), send_z, None)
    arrived = {"a_ps": ("a_ps", len(eng))}
    for n in range(3):
        arrived["a%d" % n] = ("a%d" % n, len(topo.engines(cores[peers[n]], core)))

    who = [rank] + peers
    here = [made(3) + ["psc"], ["a0", "a_ps"], ["a1", "a_ps"], ["a2", "a_ps"]]

    def sites(n, h):
        r = who[n]
        lst = T.psu if n == 0 else T.pso
        return T.zin[:, U * r:U * r + U].indirect(lst[:, 64 * r + 32 * h:64 * r + 32 * h + 32])

    for n in range(3):
        for h in range(2):
            comp("m%d_%d" % (n, h), here[n], lambda q, n=n, h=h: copy(
                q, T.mz[:, TS * n + 512 * h:TS * n + 512 * h + 512], sites(n, h)))
    early = ((0, 1, 2), (0, 2, 1), (1, 2, 0))

    def sums(q, j, lo, hi, last):
        ins = None
        for c in range(lo, hi):
            ins = q.matmul(PM[2 * j][:, 0:64], T.fin[:, TS * j + 128 * c:TS * j + 128 * c + 128],
                           T.ee[:, 7 - c:71 - c], c == 0, c == last)
        return ins

    def direct(q, j, lo, hi):
        ins = None
        for c in range(lo, hi):
            ins = q.matmul(PM[6][0:64, 0:128], T.ee[:, 7 - c:71 - c],
                           T.fin[:, TS * j + 128 * c:TS * j + 128 * c + 128], False, c == 7)
        return ins

    for j in range(3):
        a, b, c = early[j]
        pair = sorted((who[a], who[b]))
        t = [i for i in range(3) if sorted(JOINS[i][:2]) == pair or sorted(JOINS[i][2:]) == pair][0]
        mat = T.lf[:, 3, :] if sorted(JOINS[t][2:]) == pair else T.wt[:]
        for h in range(2):
            tag = "%d_%d" % (j, h)
            cols = slice(TS * j + 512 * h, TS * j + 512 * h + 512)
            bk = 2 * j + h
            comp("p" + tag, here[b] + ["m%d_%d" % (a, h)], lambda q, a=a, b=b, h=h, cols=cols: q.tensor_tensor(
                T.xj[:, cols], sites(b, h), T.mz[:, TS * a + 512 * h:TS * a + 512 * h + 512], mult))
            comp("w" + tag, ["p" + tag, "wt", free[bk]], lambda q, bk=bk, mat=mat, cols=cols: q.matmul(
                PM[bk][:], mat, T.xj[:, cols], True, True))
            comp("l" + tag, here[3] + ["m%d_%d" % (c, h)], lambda q, c=c, h=h, cols=cols: q.tensor_tensor(
                T.tmp[:, cols], sites(3, h), T.mz[:, TS * c + 512 * h:TS * c + 512 * h + 512], mult))
            cuts = [(0, 512)] if (j, h) != (2, 1) else [(0, 256), (256, 512)]
            for e, (lo, hi) in enumerate(cuts):
                at = TS * j + 512 * h
                comp("f%d_%d" % (j, h + e), ["l" + tag, "w" + tag], lambda q, bk=bk, at=at, lo=lo, hi=hi: q.tensor_tensor(
                    T.fin[:, at + lo:at + hi], PM[bk][:, lo:hi], T.tmp[:, at + lo:at + hi], mult))
        red = T.red[:, 64 * j:64 * j + 64]
        comp("rm%d_0" % j, ["f%d_0" % j, "e2"], lambda q, j=j: sums(q, j, 0, 4, 7 if j < 2 else 3))
        if j < 2:
            comp("rm%d_1" % j, ["f%d_1" % j, "rm%d_0" % j], lambda q, j=j: sums(q, j, 4, 8, 7))
            comp("rc%d" % j, ["rm%d_1" % j], lambda q, j=j, red=red: copy(q, red, PM[2 * j][:, 0:64]))
            comp("tp%d" % j, ["rc%d" % j, "id1"], lambda q, j=j, red=red: q.transpose(
                PM[2 * j + 1][0:64, 0:128], red, T.ident[:]))
            pm, ready = PM[2 * j + 1], "tp%d" % j
        else:
            comp("rc2", ["rm2_0"], lambda q, red=red: copy(q, red, PM[4][:, 0:64]))
            comp("tp2", ["rc2", "id1", free[6]], lambda q, red=red: q.matmul(
                PM[6][0:64, 0:128], red, T.ident[:], True, False))
            comp("dm0", ["f2_1", "tp2"], lambda q: direct(q, 2, 4, 6))
            comp("dm1", ["f2_2", "dm0"], lambda q: direct(q, 2, 6, 8))
            pm, ready = PM[6], "dm1"
        comp("oc%d" % j, [ready], lambda q, j=j, pm=pm: copy(q, T.outs[0:64, 128 * j:128 * j + 128], pm[0:64, 0:128]))
        dma("st%d" % j, ["oc%d" % j], [(T.y[:, TS * t:TS * t + TS], T.outs[0:64, 128 * j:128 * j + 128])], "d_y")

    order = orders()
    token, total = dict(arrived), {}
    for qn in order:
        for name in order[qn]:
            kind, deps, what, sem = ops[name]
            if kind == "c":
                total[CSEM[qn]] = total.get(CSEM[qn], 0) + 1
                token[name] = (CSEM[qn], total[CSEM[qn]])
            elif kind == "d":
                total[sem] = total.get(sem, 0) + 16 * len(what)
                token[name] = (sem, total[sem])
    for qn in order:
        q, seen = Q[qn], {}
        for name in order[qn]:
            kind, deps, what, sem = ops[name]
            need = {}
            for d in deps:
                s, val = token[d]
                if not (qn == "p" and s == "cp"):
                    need[s] = max(need.get(s, 0), val)
            for s in need:
                if seen.get(s, 0) < need[s]:
                    q.wait_ge(T.sem[s], need[s])
                    seen[s] = need[s]
            if kind == "c":
                what(q).then_inc(T.sem[CSEM[qn]], 1)
            elif kind == "d":
                for out, in_ in what:
                    q.dma_start(out, in_).then_inc(T.sem[sem], 16)
            else:
                what(q)
    g.wait_ge(T.sem.sent, sent[0])
    for s in ("cg", "cv", "cp", "cs"):
        g.wait_ge(T.sem[s], total[s])
    g.sync.wait_ge(T.sem.d_y, total["d_y"])
